import numpy as np
import ml_dtypes


def mxq(x, axis, fmt="e4m3"):
    dtype, down = {"e4m3": (ml_dtypes.float8_e4m3fn, 7), "e5m2": (ml_dtypes.float8_e5m2, 14)}[fmt]
    v = np.moveaxis(np.asarray(x, np.float32).astype(ml_dtypes.bfloat16).astype(np.float64), axis, -1)
    blocks = v.reshape(v.shape[:-1] + (-1, 32))
    amax = np.abs(blocks).max(-1, keepdims=True)
    byte = np.maximum(np.where(amax > 0, np.frexp(amax)[1] - 1 + 127, 0) - down, 1)
    scale = np.exp2(byte - 127.0)
    codes = (blocks / scale).astype(np.float32).astype(dtype).astype(np.float64)
    return np.moveaxis((codes * scale).reshape(v.shape), -1, axis)


WIDE = False


def mx_kscale(k):
    if not WIDE:
        return np.ones(k)
    levels = np.array([10, -10, 5, -5, 0])
    if k % 512:
        return np.exp2(np.random.permutation(np.resize(levels, k // 32))).repeat(32)
    a = np.empty((k // 512, 16))
    for p in range(k // 512):
        a[p, :8] = np.random.permutation(np.resize(levels, 8))
        for g in range(8):
            far = levels[np.abs(levels - a[p, g]) >= 10]
            a[p, g + 8] = far[np.random.randint(len(far))]
    return np.exp2(a.ravel()).repeat(32)


def f64(x):
    return np.asarray(x).astype(np.float64)


def striped(idx):
    return np.tile(idx.reshape(-1, 16).T, (8, 1)).astype(np.uint16)


def unstriped(offs):
    return offs[:16].T.reshape(-1).astype(np.int64)


def pack_weight(w):
    k, n = w.shape
    w = f64(np.asarray(w, np.float32).astype(ml_dtypes.bfloat16)).reshape(k // 32, 32, n)
    amax = np.abs(w).max(1)
    byte = np.clip(np.where(amax > 0, np.frexp(amax)[1] - 1 + 127 - 7, 1), 1, 254)
    scaled = (w * np.exp2(127.0 - byte)[:, None, :]).reshape(k, n).astype(np.float32)
    words = np.ascontiguousarray(scaled.reshape(k // 512, 128, 4, n).transpose(0, 1, 3, 2)).astype(ml_dtypes.float8_e4m3fn).view(np.uint8)
    return words, np.ascontiguousarray(byte.astype(np.uint8).reshape(k // 512, 16, n))


def unpack_weight(words, scales):
    g, p, n, _ = words.shape
    vals = np.ascontiguousarray(words).view(ml_dtypes.float8_e4m3fn).astype(np.float64) * np.repeat(np.exp2(scales.astype(np.float64) - 127.0), 8, axis=1)[..., None]
    return vals.transpose(0, 1, 3, 2).reshape(g * 512, n)


K, T, N, U = 1024, 512, 128, 1024


def setup_inputs():
    n = np.random.standard_normal
    s = mx_kscale(K)[:, None]
    packed_xT = pack_weight(n((K, T)) * s)
    return {
        "x_words": packed_xT[0],
        "x_scales": packed_xT[1],
        "mem": n((N, U)).astype(np.float32),
        "w1": (n((K, N)) / np.sqrt(K) / s).astype(np.float32),
        "slot": striped(np.random.permutation(U)[:T]),
    }


def reference(x_words, x_scales, mem, w1, slot):
    xq = unpack_weight(x_words, x_scales)
    y = mxq(f64(w1), 0, "e4m3").T @ xq
    out = f64(mem).copy()
    out[:, unstriped(slot)] = f64(mem)[:, unstriped(slot)] + y
    return out

@@ -1,0 +1,97 @@
+from contextlib import ExitStack
+
+import concourse.mybir as mybir
+
+K, T, N, U = 1024, 512, 128, 1024
+FLOPS = 2 * K * T * N
+
+F32 = mybir.dt.float32
+BF16 = mybir.dt.bfloat16
+I32 = mybir.dt.int32
+U32 = mybir.dt.uint32
+U16 = mybir.dt.uint16
+U8 = mybir.dt.uint8
+FP8X4 = mybir.dt.float8_e4m3fn_x4
+ADD = mybir.AluOpType.add
+
+P = 128
+PACK = 4
+PASSES = K // (P * PACK)
+HEAD = 128
+GROUP = 128
+
+
+def tile_picked_widxput_add_l_kernel(tc, x_words, x_scales, mem, w1, slot, out):
+    nc = tc.nc
+    with ExitStack() as ctx:
+        keep = ctx.enter_context(tc.tile_pool(name="keep", bufs=1))
+        psum = ctx.enter_context(tc.psum_pool(name="psum", bufs=1))
+
+        offsets = keep.tile([P, T // 16], U16, name="offsets")
+        store = keep.tile([P, U], F32, name="store")
+        x_planes = keep.tile([P, T], U8, name="x_planes", align_bytes=64)
+        x_head = keep.tile([P, PASSES, HEAD], U32, name="x_head", align_bytes=64)
+        x_rest = keep.tile([P, PASSES, T - HEAD], U32, name="x_rest", align_bytes=64)
+        w_raw = [keep.tile([P, PACK, N], F32, name="w_raw%d" % z) for z in range(PASSES)]
+        w_grouped = [keep.tile([P, N, PACK], BF16, name="w_grouped%d" % z, align_bytes=64) for z in range(PASSES)]
+        w_codes = [keep.tile([P, N], U32, name="w_codes%d" % z, align_bytes=64) for z in range(PASSES)]
+        w_scales = [keep.tile([P, N], U8, name="w_scales%d" % z, align_bytes=64) for z in range(PASSES)]
+        old_head = keep.tile([P, HEAD], F32, name="old_head")
+        old_rest = keep.tile([P, T - HEAD], F32, name="old_rest")
+        new_head = keep.tile([P, HEAD], F32, name="new_head")
+        new_rest = keep.tile([P, T - HEAD], F32, name="new_rest")
+        y_head = psum.tile([P, HEAD], F32, name="y_head")
+        y_rest = psum.tile([P, T - HEAD], F32, name="y_rest")
+
+        nc.vector.memset(x_planes[:].bitcast(I32), 0)
+
+        w_rows = w1.rearrange("(z p j) m -> z p j m", p=P, j=PACK)
+        for z in range(PASSES):
+            nc.sync.dma_start(out=w_raw[z][:], in_=w_rows[z])
+        nc.sync.dma_start(offsets[:], slot)
+        nc.sync.dma_start(out=store[:], in_=mem)
+        for q in range(4):
+            nc.sync.dma_start(
+                out=x_planes[32 * q : 32 * q + 4 * PASSES, :].bitcast(I32),
+                in_=x_scales[:, 4 * q : 4 * q + 4, :].bitcast(I32),
+            )
+        x_rows = x_words.rearrange("z p c r -> p z (c r)")
+        nc.sync.dma_start(out=x_head[:].bitcast(I32), in_=x_rows[:, :, : PACK * HEAD].bitcast(I32))
+        nc.sync.dma_start(out=x_rest[:].bitcast(I32), in_=x_rows[:, :, PACK * HEAD :].bitcast(I32))
+
+        for z in range(PASSES):
+            nc.vector.tensor_copy(out=w_grouped[z][:], in_=w_raw[z][:].rearrange("p j m -> p m j"))
+        for z in range(PASSES):
+            nc.vector.quantize_mx(
+                out=w_codes[z][:].bitcast(FP8X4),
+                scales=w_scales[z][:],
+                in_=w_grouped[z][:].rearrange("p m j -> p (m j)"),
+            )
+
+        def project(y, words, first):
+            for c in range(0, y.shape[1], GROUP):
+                for z in range(PASSES):
+                    nc.tensor.matmul_mx(
+                        out=y[:, c : c + GROUP],
+                        lhsT=w_codes[z][:].bitcast(FP8X4),
+                        lhsT_scale=w_scales[z][:],
+                        rhs=words[:, z, c : c + GROUP].bitcast(FP8X4),
+                        rhs_scale=x_planes[4 * z :, first + c : first + c + GROUP],
+                        start=(z == 0),
+                        stop=(z == PASSES - 1),
+                    )
+
+        def listed(first, count):
+            return store[:].indirect(offsets[:, first // 16 : (first + count) // 16])
+
+        project(y_head, x_head, 0)
+        project(y_rest, x_rest, HEAD)
+
+        nc.vector.tensor_copy(old_head[:], listed(0, HEAD))
+        nc.vector.tensor_copy(old_rest[:, :256], listed(HEAD, 256))
+        nc.vector.tensor_tensor(new_head[:], y_head[:], old_head[:], ADD)
+        nc.vector.tensor_copy(old_rest[:, 256:], listed(HEAD + 256, 128))
+        nc.vector.tensor_copy(listed(0, HEAD), new_head[:])
+        nc.vector.tensor_tensor(new_rest[:], y_rest[:], old_rest[:], ADD)
+        nc.vector.tensor_copy(listed(HEAD, T - HEAD), new_rest[:])
+        nc.sync.dma_start(out=out, in_=store[:])

@@ -18,7 +18,8 @@ P = 128
 PACK = 4
 PASSES = K // (P * PACK)
 HEAD = 128
-GROUP = 128
+BODY = 256
+TAIL = 128
 
 
 def tile_picked_widxput_add_l_kernel(tc, x_words, x_scales, mem, w1, slot, out):
@@ -29,38 +30,40 @@ def tile_picked_widxput_add_l_kernel(tc, x_words, x_scales, mem, w1, slot, out):
 
         offsets = keep.tile([P, T // 16], U16, name="offsets")
         store = keep.tile([P, U], F32, name="store")
+        table = keep.tile([P, U], F32, name="table")
+        warm = keep.tile([P, 16], F32, name="warm")
         x_planes = keep.tile([P, T], U8, name="x_planes", align_bytes=64)
-        x_head = keep.tile([P, PASSES, HEAD], U32, name="x_head", align_bytes=64)
+        x_head = keep.tile([P, PASSES, HEAD], U32, name="x_head", tag="turns", align_bytes=64)
         x_rest = keep.tile([P, PASSES, T - HEAD], U32, name="x_rest", align_bytes=64)
-        w_raw = [keep.tile([P, PACK, N], F32, name="w_raw%d" % z) for z in range(PASSES)]
+        w_raw = keep.tile([P, PASSES, PACK, N], F32, name="w_raw")
         w_grouped = [keep.tile([P, N, PACK], BF16, name="w_grouped%d" % z, align_bytes=64) for z in range(PASSES)]
         w_codes = [keep.tile([P, N], U32, name="w_codes%d" % z, align_bytes=64) for z in range(PASSES)]
         w_scales = [keep.tile([P, N], U8, name="w_scales%d" % z, align_bytes=64) for z in range(PASSES)]
-        old_head = keep.tile([P, HEAD], F32, name="old_head")
-        old_rest = keep.tile([P, T - HEAD], F32, name="old_rest")
+        old = keep.tile([P, HEAD + BODY], F32, name="old")
         new_head = keep.tile([P, HEAD], F32, name="new_head")
         new_rest = keep.tile([P, T - HEAD], F32, name="new_rest")
         y_head = psum.tile([P, HEAD], F32, name="y_head")
-        y_rest = psum.tile([P, T - HEAD], F32, name="y_rest")
+        y_body = psum.tile([P, BODY], F32, name="y_body")
+        y_tail = psum.tile([P, TAIL], F32, name="y_tail")
 
         nc.vector.memset(x_planes[:].bitcast(I32), 0)
+        nc.gpsimd.memset(warm[:, :8], 0.0)
+        nc.scalar.copy(warm[:, 8:], warm[:, :8])
 
-        w_rows = w1.rearrange("(z p j) m -> z p j m", p=P, j=PACK)
-        for z in range(PASSES):
-            nc.sync.dma_start(out=w_raw[z][:], in_=w_rows[z])
+        x_rows = x_words.rearrange("z p c r -> p z (c r)")
         nc.sync.dma_start(offsets[:], slot)
-        nc.sync.dma_start(out=store[:], in_=mem)
+        nc.sync.dma_start(out=w_raw[:], in_=w1.rearrange("(z p j) m -> p z j m", p=P, j=PACK))
+        nc.sync.dma_start(out=table[:], in_=mem)
         for q in range(4):
             nc.sync.dma_start(
                 out=x_planes[32 * q : 32 * q + 4 * PASSES, :].bitcast(I32),
                 in_=x_scales[:, 4 * q : 4 * q + 4, :].bitcast(I32),
             )
-        x_rows = x_words.rearrange("z p c r -> p z (c r)")
         nc.sync.dma_start(out=x_head[:].bitcast(I32), in_=x_rows[:, :, : PACK * HEAD].bitcast(I32))
         nc.sync.dma_start(out=x_rest[:].bitcast(I32), in_=x_rows[:, :, PACK * HEAD :].bitcast(I32))
 
-        for z in range(PASSES):
-            nc.vector.tensor_copy(out=w_grouped[z][:], in_=w_raw[z][:].rearrange("p j m -> p m j"))
+        nc.vector.tensor_copy(out=w_grouped[0][:], in_=w_raw[:, 0].rearrange("p j m -> p m j"))
+        nc.scalar.copy(out=w_grouped[1][:], in_=w_raw[:, 1].rearrange("p j m -> p m j"))
         for z in range(PASSES):
             nc.vector.quantize_mx(
                 out=w_codes[z][:].bitcast(FP8X4),
@@ -68,30 +71,37 @@ def tile_picked_widxput_add_l_kernel(tc, x_words, x_scales, mem, w1, slot, out):
                 in_=w_grouped[z][:].rearrange("p m j -> p (m j)"),
             )
 
-        def project(y, words, first):
-            for c in range(0, y.shape[1], GROUP):
-                for z in range(PASSES):
-                    nc.tensor.matmul_mx(
-                        out=y[:, c : c + GROUP],
-                        lhsT=w_codes[z][:].bitcast(FP8X4),
-                        lhsT_scale=w_scales[z][:],
-                        rhs=words[:, z, c : c + GROUP].bitcast(FP8X4),
-                        rhs_scale=x_planes[4 * z :, first + c : first + c + GROUP],
-                        start=(z == 0),
-                        stop=(z == PASSES - 1),
-                    )
+        def project(y, words, at, first):
+            width = y.shape[1]
+            for z in range(PASSES):
+                nc.tensor.matmul_mx(
+                    out=y[:],
+                    lhsT=w_codes[z][:].bitcast(FP8X4),
+                    lhsT_scale=w_scales[z][:],
+                    rhs=words[:, z, at : at + width].bitcast(FP8X4),
+                    rhs_scale=x_planes[4 * z :, first : first + width],
+                    start=(z == 0),
+                    stop=(z == PASSES - 1),
+                )
 
         def listed(first, count):
             return store[:].indirect(offsets[:, first // 16 : (first + count) // 16])
 
-        project(y_head, x_head, 0)
-        project(y_rest, x_rest, HEAD)
+        def looked_up(first, count):
+            return table[:].indirect(offsets[:, first // 16 : (first + count) // 16])
 
-        nc.vector.tensor_copy(old_head[:], listed(0, HEAD))
-        nc.vector.tensor_copy(old_rest[:, :256], listed(HEAD, 256))
-        nc.vector.tensor_tensor(new_head[:], y_head[:], old_head[:], ADD)
-        nc.vector.tensor_copy(old_rest[:, 256:], listed(HEAD + 256, 128))
+        project(y_head, x_head, 0, 0)
+        project(y_body, x_rest, 0, HEAD)
+        project(y_tail, x_rest, BODY, HEAD + BODY)
+
+        nc.scalar.copy(store[:], table[:])
+        nc.vector.tensor_copy(old[:, :HEAD], looked_up(0, HEAD))
+        nc.vector.tensor_copy(old[:, HEAD:], looked_up(HEAD, BODY))
+        nc.vector.tensor_tensor(new_head[:], y_head[:], old[:, :HEAD], ADD)
+        old_tail = keep.tile([P, TAIL], F32, name="old_tail", tag="turns", align_bytes=64)
+        nc.vector.tensor_copy(old_tail[:], looked_up(HEAD + BODY, TAIL))
         nc.vector.tensor_copy(listed(0, HEAD), new_head[:])
-        nc.vector.tensor_tensor(new_rest[:], y_rest[:], old_rest[:], ADD)
+        nc.vector.tensor_tensor(new_rest[:, :BODY], y_body[:], old[:, HEAD:], ADD)
+        nc.vector.tensor_tensor(new_rest[:, BODY:], y_tail[:], old_tail[:], ADD)
         nc.vector.tensor_copy(listed(HEAD, T - HEAD), new_rest[:])
         nc.sync.dma_start(out=out, in_=store[:])

@@ -33,15 +33,16 @@ def tile_picked_widxput_add_l_kernel(tc, x_words, x_scales, mem, w1, slot, out):
         table = keep.tile([P, U], F32, name="table")
         warm = keep.tile([P, 16], F32, name="warm")
         x_planes = keep.tile([P, T], U8, name="x_planes", align_bytes=64)
-        x_head = keep.tile([P, PASSES, HEAD], U32, name="x_head", tag="turns", align_bytes=64)
+        x_head = keep.tile([P, PASSES, HEAD], U32, name="x_head", align_bytes=64)
         x_rest = keep.tile([P, PASSES, T - HEAD], U32, name="x_rest", align_bytes=64)
         w_raw = keep.tile([P, PASSES, PACK, N], F32, name="w_raw")
         w_grouped = [keep.tile([P, N, PACK], BF16, name="w_grouped%d" % z, align_bytes=64) for z in range(PASSES)]
         w_codes = [keep.tile([P, N], U32, name="w_codes%d" % z, align_bytes=64) for z in range(PASSES)]
         w_scales = [keep.tile([P, N], U8, name="w_scales%d" % z, align_bytes=64) for z in range(PASSES)]
-        old = keep.tile([P, HEAD + BODY], F32, name="old")
-        new_head = keep.tile([P, HEAD], F32, name="new_head")
-        new_rest = keep.tile([P, T - HEAD], F32, name="new_rest")
+        old_head = keep.tile([P, HEAD], F32, name="old_head")
+        old_rest = keep.tile([P, T - HEAD], F32, name="old_rest")
+        add_head = keep.tile([P, HEAD], F32, name="add_head")
+        add_rest = keep.tile([P, T - HEAD], F32, name="add_rest")
         y_head = psum.tile([P, HEAD], F32, name="y_head")
         y_body = psum.tile([P, BODY], F32, name="y_body")
         y_tail = psum.tile([P, TAIL], F32, name="y_tail")
@@ -95,13 +96,11 @@ def tile_picked_widxput_add_l_kernel(tc, x_words, x_scales, mem, w1, slot, out):
         project(y_tail, x_rest, BODY, HEAD + BODY)
 
         nc.scalar.copy(store[:], table[:])
-        nc.vector.tensor_copy(old[:, :HEAD], looked_up(0, HEAD))
-        nc.vector.tensor_copy(old[:, HEAD:], looked_up(HEAD, BODY))
-        nc.vector.tensor_tensor(new_head[:], y_head[:], old[:, :HEAD], ADD)
-        old_tail = keep.tile([P, TAIL], F32, name="old_tail", tag="turns", align_bytes=64)
-        nc.vector.tensor_copy(old_tail[:], looked_up(HEAD + BODY, TAIL))
-        nc.vector.tensor_copy(listed(0, HEAD), new_head[:])
-        nc.vector.tensor_tensor(new_rest[:, :BODY], y_body[:], old[:, HEAD:], ADD)
-        nc.vector.tensor_tensor(new_rest[:, BODY:], y_tail[:], old_tail[:], ADD)
-        nc.vector.tensor_copy(listed(HEAD, T - HEAD), new_rest[:])
+        nc.vector.tensor_copy(old_head[:], looked_up(0, HEAD))
+        nc.vector.tensor_copy(old_rest[:], looked_up(HEAD, T - HEAD))
+        nc.scalar.copy(add_head[:], y_head[:])
+        nc.scalar.copy(add_rest[:, :BODY], y_body[:])
+        nc.scalar.copy(add_rest[:, BODY:], y_tail[:])
+        nc.vector.tensor_tensor(listed(0, HEAD), old_head[:], add_head[:], ADD)
+        nc.vector.tensor_tensor(listed(HEAD, T - HEAD), old_rest[:], add_rest[:], ADD)
         nc.sync.dma_start(out=out, in_=store[:])

@@ -17,9 +17,10 @@ ADD = mybir.AluOpType.add
 P = 128
 PACK = 4
 PASSES = K // (P * PACK)
+PIECE = 128
 HEAD = 128
-BODY = 256
-TAIL = 128
+SCALAR_COPY = 896
+X_LOADS = ((0, 128), (128, 256), (384, 128))
 
 
 def tile_picked_widxput_add_l_kernel(tc, x_words, x_scales, mem, w1, slot, out):
@@ -33,8 +34,9 @@ def tile_picked_widxput_add_l_kernel(tc, x_words, x_scales, mem, w1, slot, out):
         table = keep.tile([P, U], F32, name="table")
         warm = keep.tile([P, 16], F32, name="warm")
         x_planes = keep.tile([P, T], U8, name="x_planes", align_bytes=64)
-        x_head = keep.tile([P, PASSES, HEAD], U32, name="x_head", align_bytes=64)
-        x_rest = keep.tile([P, PASSES, T - HEAD], U32, name="x_rest", align_bytes=64)
+        x_parts = [
+            keep.tile([P, PASSES, width], U32, name="x_part%d" % first, align_bytes=64) for first, width in X_LOADS
+        ]
         w_raw = keep.tile([P, PASSES, PACK, N], F32, name="w_raw")
         w_grouped = [keep.tile([P, N, PACK], BF16, name="w_grouped%d" % z, align_bytes=64) for z in range(PASSES)]
         w_codes = [keep.tile([P, N], U32, name="w_codes%d" % z, align_bytes=64) for z in range(PASSES)]
@@ -43,9 +45,7 @@ def tile_picked_widxput_add_l_kernel(tc, x_words, x_scales, mem, w1, slot, out):
         old_rest = keep.tile([P, T - HEAD], F32, name="old_rest")
         add_head = keep.tile([P, HEAD], F32, name="add_head")
         add_rest = keep.tile([P, T - HEAD], F32, name="add_rest")
-        y_head = psum.tile([P, HEAD], F32, name="y_head")
-        y_body = psum.tile([P, BODY], F32, name="y_body")
-        y_tail = psum.tile([P, TAIL], F32, name="y_tail")
+        y = [psum.tile([P, PIECE], F32, name="y%d" % i) for i in range(T // PIECE)]
 
         nc.vector.memset(x_planes[:].bitcast(I32), 0)
         nc.gpsimd.memset(warm[:, :8], 0.0)
@@ -60,8 +60,11 @@ def tile_picked_widxput_add_l_kernel(tc, x_words, x_scales, mem, w1, slot, out):
                 out=x_planes[32 * q : 32 * q + 4 * PASSES, :].bitcast(I32),
                 in_=x_scales[:, 4 * q : 4 * q + 4, :].bitcast(I32),
             )
-        nc.sync.dma_start(out=x_head[:].bitcast(I32), in_=x_rows[:, :, : PACK * HEAD].bitcast(I32))
-        nc.sync.dma_start(out=x_rest[:].bitcast(I32), in_=x_rows[:, :, PACK * HEAD :].bitcast(I32))
+        for part, (first, width) in zip(x_parts, X_LOADS):
+            nc.sync.dma_start(
+                out=part[:].bitcast(I32),
+                in_=x_rows[:, :, PACK * first : PACK * (first + width)].bitcast(I32),
+            )
 
         nc.vector.tensor_copy(out=w_grouped[0][:], in_=w_raw[:, 0].rearrange("p j m -> p m j"))
         nc.scalar.copy(out=w_grouped[1][:], in_=w_raw[:, 1].rearrange("p j m -> p m j"))
@@ -72,11 +75,11 @@ def tile_picked_widxput_add_l_kernel(tc, x_words, x_scales, mem, w1, slot, out):
                 in_=w_grouped[z][:].rearrange("p m j -> p (m j)"),
             )
 
-        def project(y, words, at, first):
-            width = y.shape[1]
+        def project(acc, words, at, first):
+            width = acc.shape[1]
             for z in range(PASSES):
                 nc.tensor.matmul_mx(
-                    out=y[:],
+                    out=acc[:],
                     lhsT=w_codes[z][:].bitcast(FP8X4),
                     lhsT_scale=w_scales[z][:],
                     rhs=words[:, z, at : at + width].bitcast(FP8X4),
@@ -91,16 +94,17 @@ def tile_picked_widxput_add_l_kernel(tc, x_words, x_scales, mem, w1, slot, out):
         def looked_up(first, count):
             return table[:].indirect(offsets[:, first // 16 : (first + count) // 16])
 
-        project(y_head, x_head, 0, 0)
-        project(y_body, x_rest, 0, HEAD)
-        project(y_tail, x_rest, BODY, HEAD + BODY)
+        for part, (first, width) in zip(x_parts, X_LOADS):
+            for at in range(0, width, PIECE):
+                project(y[(first + at) // PIECE], part, at, first + at)
 
-        nc.scalar.copy(store[:], table[:])
+        nc.vector.tensor_copy(store[:, SCALAR_COPY:], table[:, SCALAR_COPY:])
+        nc.scalar.copy(store[:, :SCALAR_COPY], table[:, :SCALAR_COPY])
         nc.vector.tensor_copy(old_head[:], looked_up(0, HEAD))
         nc.vector.tensor_copy(old_rest[:], looked_up(HEAD, T - HEAD))
-        nc.scalar.copy(add_head[:], y_head[:])
-        nc.scalar.copy(add_rest[:, :BODY], y_body[:])
-        nc.scalar.copy(add_rest[:, BODY:], y_tail[:])
+        nc.scalar.copy(add_head[:], y[0][:])
+        for i in range(1, T // PIECE):
+            nc.scalar.copy(add_rest[:, (i - 1) * PIECE : i * PIECE], y[i][:])
         nc.vector.tensor_tensor(listed(0, HEAD), old_head[:], add_head[:], ADD)
         nc.vector.tensor_tensor(listed(HEAD, T - HEAD), old_rest[:], add_rest[:], ADD)
         nc.sync.dma_start(out=out, in_=store[:])

@@ -20,7 +20,6 @@ PASSES = K // (P * PACK)
 PIECE = 128
 HEAD = 128
 SCALAR_COPY = 896
-X_LOADS = ((0, 128), (128, 256), (384, 128))
 
 
 def tile_picked_widxput_add_l_kernel(tc, x_words, x_scales, mem, w1, slot, out):
@@ -34,9 +33,8 @@ def tile_picked_widxput_add_l_kernel(tc, x_words, x_scales, mem, w1, slot, out):
         table = keep.tile([P, U], F32, name="table")
         warm = keep.tile([P, 16], F32, name="warm")
         x_planes = keep.tile([P, T], U8, name="x_planes", align_bytes=64)
-        x_parts = [
-            keep.tile([P, PASSES, width], U32, name="x_part%d" % first, align_bytes=64) for first, width in X_LOADS
-        ]
+        x_head = keep.tile([P, PASSES, HEAD], U32, name="x_head", align_bytes=64)
+        x_rest = [keep.tile([P, T - HEAD], U32, name="x_rest%d" % z, align_bytes=64) for z in range(PASSES)]
         w_raw = keep.tile([P, PASSES, PACK, N], F32, name="w_raw")
         w_grouped = [keep.tile([P, N, PACK], BF16, name="w_grouped%d" % z, align_bytes=64) for z in range(PASSES)]
         w_codes = [keep.tile([P, N], U32, name="w_codes%d" % z, align_bytes=64) for z in range(PASSES)]
@@ -60,11 +58,9 @@ def tile_picked_widxput_add_l_kernel(tc, x_words, x_scales, mem, w1, slot, out):
                 out=x_planes[32 * q : 32 * q + 4 * PASSES, :].bitcast(I32),
                 in_=x_scales[:, 4 * q : 4 * q + 4, :].bitcast(I32),
             )
-        for part, (first, width) in zip(x_parts, X_LOADS):
-            nc.sync.dma_start(
-                out=part[:].bitcast(I32),
-                in_=x_rows[:, :, PACK * first : PACK * (first + width)].bitcast(I32),
-            )
+        nc.sync.dma_start(out=x_head[:].bitcast(I32), in_=x_rows[:, :, : PACK * HEAD].bitcast(I32))
+        for z in range(PASSES):
+            nc.sync.dma_start(out=x_rest[z][:].bitcast(I32), in_=x_rows[:, z, PACK * HEAD :].bitcast(I32))
 
         nc.vector.tensor_copy(out=w_grouped[0][:], in_=w_raw[:, 0].rearrange("p j m -> p m j"))
         nc.scalar.copy(out=w_grouped[1][:], in_=w_raw[:, 1].rearrange("p j m -> p m j"))
@@ -75,18 +71,16 @@ def tile_picked_widxput_add_l_kernel(tc, x_words, x_scales, mem, w1, slot, out):
                 in_=w_grouped[z][:].rearrange("p m j -> p (m j)"),
             )
 
-        def project(acc, words, at, first):
-            width = acc.shape[1]
-            for z in range(PASSES):
-                nc.tensor.matmul_mx(
-                    out=acc[:],
-                    lhsT=w_codes[z][:].bitcast(FP8X4),
-                    lhsT_scale=w_scales[z][:],
-                    rhs=words[:, z, at : at + width].bitcast(FP8X4),
-                    rhs_scale=x_planes[4 * z :, first : first + width],
-                    start=(z == 0),
-                    stop=(z == PASSES - 1),
-                )
+        def project(piece, z, words):
+            nc.tensor.matmul_mx(
+                out=y[piece][:],
+                lhsT=w_codes[z][:].bitcast(FP8X4),
+                lhsT_scale=w_scales[z][:],
+                rhs=words.bitcast(FP8X4),
+                rhs_scale=x_planes[4 * z :, piece * PIECE : (piece + 1) * PIECE],
+                start=(z == 0),
+                stop=(z == PASSES - 1),
+            )
 
         def listed(first, count):
             return store[:].indirect(offsets[:, first // 16 : (first + count) // 16])
@@ -94,9 +88,11 @@ def tile_picked_widxput_add_l_kernel(tc, x_words, x_scales, mem, w1, slot, out):
         def looked_up(first, count):
             return table[:].indirect(offsets[:, first // 16 : (first + count) // 16])
 
-        for part, (first, width) in zip(x_parts, X_LOADS):
-            for at in range(0, width, PIECE):
-                project(y[(first + at) // PIECE], part, at, first + at)
+        for z in range(PASSES):
+            project(0, z, x_head[:, z, :])
+        for z in range(PASSES):
+            for i in range(1, T // PIECE):
+                project(i, z, x_rest[z][:, (i - 1) * PIECE : i * PIECE])
 
         nc.vector.tensor_copy(store[:, SCALAR_COPY:], table[:, SCALAR_COPY:])
         nc.scalar.copy(store[:, :SCALAR_COPY], table[:, :SCALAR_COPY])

@@ -33,7 +33,7 @@ def tile_picked_widxput_add_l_kernel(tc, x_words, x_scales, mem, w1, slot, out):
         table = keep.tile([P, U], F32, name="table")
         warm = keep.tile([P, 16], F32, name="warm")
         x_planes = keep.tile([P, T], U8, name="x_planes", align_bytes=64)
-        x_head = keep.tile([P, PASSES, HEAD], U32, name="x_head", align_bytes=64)
+        x_head = [keep.tile([P, HEAD], U32, name="x_head%d" % z, align_bytes=64) for z in range(PASSES)]
         x_rest = [keep.tile([P, T - HEAD], U32, name="x_rest%d" % z, align_bytes=64) for z in range(PASSES)]
         w_raw = keep.tile([P, PASSES, PACK, N], F32, name="w_raw")
         w_grouped = [keep.tile([P, N, PACK], BF16, name="w_grouped%d" % z, align_bytes=64) for z in range(PASSES)]
@@ -50,6 +50,7 @@ def tile_picked_widxput_add_l_kernel(tc, x_words, x_scales, mem, w1, slot, out):
         nc.scalar.copy(warm[:, 8:], warm[:, :8])
 
         x_rows = x_words.rearrange("z p c r -> p z (c r)")
+        nc.sync.dma_start(out=x_head[0][:].bitcast(I32), in_=x_rows[:, 0, : PACK * HEAD].bitcast(I32))
         nc.sync.dma_start(offsets[:], slot)
         nc.sync.dma_start(out=w_raw[:], in_=w1.rearrange("(z p j) m -> p z j m", p=P, j=PACK))
         nc.sync.dma_start(out=table[:], in_=mem)
@@ -58,7 +59,7 @@ def tile_picked_widxput_add_l_kernel(tc, x_words, x_scales, mem, w1, slot, out):
                 out=x_planes[32 * q : 32 * q + 4 * PASSES, :].bitcast(I32),
                 in_=x_scales[:, 4 * q : 4 * q + 4, :].bitcast(I32),
             )
-        nc.sync.dma_start(out=x_head[:].bitcast(I32), in_=x_rows[:, :, : PACK * HEAD].bitcast(I32))
+        nc.sync.dma_start(out=x_head[1][:].bitcast(I32), in_=x_rows[:, 1, : PACK * HEAD].bitcast(I32))
         for z in range(PASSES):
             nc.sync.dma_start(out=x_rest[z][:].bitcast(I32), in_=x_rows[:, z, PACK * HEAD :].bitcast(I32))
 
@@ -89,7 +90,7 @@ def tile_picked_widxput_add_l_kernel(tc, x_words, x_scales, mem, w1, slot, out):
             return table[:].indirect(offsets[:, first // 16 : (first + count) // 16])
 
         for z in range(PASSES):
-            project(0, z, x_head[:, z, :])
+            project(0, z, x_head[z][:])
         for z in range(PASSES):
             for i in range(1, T // PIECE):
                 project(i, z, x_rest[z][:, (i - 1) * PIECE : i * PIECE])

@@ -20,6 +20,7 @@ PASSES = K // (P * PACK)
 PIECE = 128
 HEAD = 128
 SCALAR_COPY = 896
+VECTOR_CAST = 48
 
 
 def tile_picked_widxput_add_l_kernel(tc, x_words, x_scales, mem, w1, slot, out):
@@ -64,7 +65,8 @@ def tile_picked_widxput_add_l_kernel(tc, x_words, x_scales, mem, w1, slot, out):
             nc.sync.dma_start(out=x_rest[z][:].bitcast(I32), in_=x_rows[:, z, PACK * HEAD :].bitcast(I32))
 
         nc.vector.tensor_copy(out=w_grouped[0][:], in_=w_raw[:, 0].rearrange("p j m -> p m j"))
-        nc.scalar.copy(out=w_grouped[1][:], in_=w_raw[:, 1].rearrange("p j m -> p m j"))
+        nc.vector.tensor_copy(out=w_grouped[1][:, :VECTOR_CAST], in_=w_raw[:, 1, :, :VECTOR_CAST].rearrange("p j m -> p m j"))
+        nc.scalar.copy(out=w_grouped[1][:, VECTOR_CAST:], in_=w_raw[:, 1, :, VECTOR_CAST:].rearrange("p j m -> p m j"))
         for z in range(PASSES):
             nc.vector.quantize_mx(
                 out=w_codes[z][:].bitcast(FP8X4),

@@ -27,28 +27,23 @@ def tile_picked_widxput_add_l_kernel(tc, x_words, x_scales, mem, w1, slot, out):
     nc = tc.nc
     with ExitStack() as ctx:
         keep = ctx.enter_context(tc.tile_pool(name="keep", bufs=1))
+        stage = ctx.enter_context(tc.tile_pool(name="stage", bufs=1))
         psum = ctx.enter_context(tc.psum_pool(name="psum", bufs=1))
 
         offsets = keep.tile([P, T // 16], U16, name="offsets")
-        store = keep.tile([P, U], F32, name="store")
         table = keep.tile([P, U], F32, name="table")
-        warm = keep.tile([P, 16], F32, name="warm")
         x_planes = keep.tile([P, T], U8, name="x_planes", align_bytes=64)
         x_head = [keep.tile([P, HEAD], U32, name="x_head%d" % z, align_bytes=64) for z in range(PASSES)]
         x_rest = [keep.tile([P, T - HEAD], U32, name="x_rest%d" % z, align_bytes=64) for z in range(PASSES)]
-        w_raw = keep.tile([P, PASSES, PACK, N], F32, name="w_raw")
+        w_raw = stage.tile([P, PASSES, PACK, N], F32, name="w_raw", offset=2 * T)
         w_grouped = [keep.tile([P, N, PACK], BF16, name="w_grouped%d" % z, align_bytes=64) for z in range(PASSES)]
         w_codes = [keep.tile([P, N], U32, name="w_codes%d" % z, align_bytes=64) for z in range(PASSES)]
         w_scales = [keep.tile([P, N], U8, name="w_scales%d" % z, align_bytes=64) for z in range(PASSES)]
-        old_head = keep.tile([P, HEAD], F32, name="old_head")
-        old_rest = keep.tile([P, T - HEAD], F32, name="old_rest")
         add_head = keep.tile([P, HEAD], F32, name="add_head")
         add_rest = keep.tile([P, T - HEAD], F32, name="add_rest")
         y = [psum.tile([P, PIECE], F32, name="y%d" % i) for i in range(T // PIECE)]
 
         nc.vector.memset(x_planes[:].bitcast(I32), 0)
-        nc.gpsimd.memset(warm[:, :8], 0.0)
-        nc.scalar.copy(warm[:, 8:], warm[:, :8])
 
         x_rows = x_words.rearrange("z p c r -> p z (c r)")
         nc.sync.dma_start(out=x_head[0][:].bitcast(I32), in_=x_rows[:, 0, : PACK * HEAD].bitcast(I32))
@@ -97,8 +92,11 @@ def tile_picked_widxput_add_l_kernel(tc, x_words, x_scales, mem, w1, slot, out):
             for i in range(1, T // PIECE):
                 project(i, z, x_rest[z][:, (i - 1) * PIECE : i * PIECE])
 
+        store = stage.tile([P, U], F32, name="store", offset=4 * T)
         nc.vector.tensor_copy(store[:, SCALAR_COPY:], table[:, SCALAR_COPY:])
         nc.scalar.copy(store[:, :SCALAR_COPY], table[:, :SCALAR_COPY])
+        old_head = stage.tile([P, HEAD], F32, name="old_head", offset=4 * (T - HEAD))
+        old_rest = stage.tile([P, T - HEAD], F32, name="old_rest", offset=0)
         nc.vector.tensor_copy(old_head[:], looked_up(0, HEAD))
         nc.vector.tensor_copy(old_rest[:], looked_up(HEAD, T - HEAD))
         nc.scalar.copy(add_head[:], y[0][:])

@@ -19,8 +19,9 @@ PACK = 4
 PASSES = K // (P * PACK)
 PIECE = 128
 HEAD = 128
-SCALAR_COPY = 896
-VECTOR_CAST = 48
+SCALAR_COPY = 832
+VECTOR_CAST = 96
+LINE = 4
 
 
 def tile_picked_widxput_add_l_kernel(tc, x_words, x_scales, mem, w1, slot, out):
@@ -59,9 +60,12 @@ def tile_picked_widxput_add_l_kernel(tc, x_words, x_scales, mem, w1, slot, out):
         for z in range(PASSES):
             nc.sync.dma_start(out=x_rest[z][:].bitcast(I32), in_=x_rows[:, z, PACK * HEAD :].bitcast(I32))
 
-        nc.vector.tensor_copy(out=w_grouped[0][:], in_=w_raw[:, 0].rearrange("p j m -> p m j"))
-        nc.vector.tensor_copy(out=w_grouped[1][:, :VECTOR_CAST], in_=w_raw[:, 1, :, :VECTOR_CAST].rearrange("p j m -> p m j"))
-        nc.scalar.copy(out=w_grouped[1][:, VECTOR_CAST:], in_=w_raw[:, 1, :, VECTOR_CAST:].rearrange("p j m -> p m j"))
+        for z in range(PASSES):
+            for copy, cols in ((nc.vector.tensor_copy, slice(0, VECTOR_CAST)), (nc.scalar.copy, slice(VECTOR_CAST, N))):
+                copy(
+                    out=w_grouped[z][:, cols].rearrange("p (c i) j -> p c j i", i=LINE),
+                    in_=w_raw[:, z, :, cols].rearrange("p j (c i) -> p c j i", i=LINE),
+                )
         for z in range(PASSES):
             nc.vector.quantize_mx(
                 out=w_codes[z][:].bitcast(FP8X4),

@@ -22,6 +22,7 @@ HEAD = 128
 SCALAR_COPY = 832
 VECTOR_CAST = 96
 LINE = 4
+ALIGN = 256
 
 
 def tile_picked_widxput_add_l_kernel(tc, x_words, x_scales, mem, w1, slot, out):
@@ -31,17 +32,17 @@ def tile_picked_widxput_add_l_kernel(tc, x_words, x_scales, mem, w1, slot, out):
         stage = ctx.enter_context(tc.tile_pool(name="stage", bufs=1))
         psum = ctx.enter_context(tc.psum_pool(name="psum", bufs=1))
 
-        offsets = keep.tile([P, T // 16], U16, name="offsets")
-        table = keep.tile([P, U], F32, name="table")
-        x_planes = keep.tile([P, T], U8, name="x_planes", align_bytes=64)
-        x_head = [keep.tile([P, HEAD], U32, name="x_head%d" % z, align_bytes=64) for z in range(PASSES)]
-        x_rest = [keep.tile([P, T - HEAD], U32, name="x_rest%d" % z, align_bytes=64) for z in range(PASSES)]
-        w_raw = stage.tile([P, PASSES, PACK, N], F32, name="w_raw", offset=2 * T)
-        w_grouped = [keep.tile([P, N, PACK], BF16, name="w_grouped%d" % z, align_bytes=64) for z in range(PASSES)]
-        w_codes = [keep.tile([P, N], U32, name="w_codes%d" % z, align_bytes=64) for z in range(PASSES)]
-        w_scales = [keep.tile([P, N], U8, name="w_scales%d" % z, align_bytes=64) for z in range(PASSES)]
-        add_head = keep.tile([P, HEAD], F32, name="add_head")
-        add_rest = keep.tile([P, T - HEAD], F32, name="add_rest")
+        offsets = keep.tile([P, T // 16], U16, name="offsets", align_bytes=ALIGN)
+        table = keep.tile([P, U], F32, name="table", align_bytes=ALIGN)
+        x_planes = keep.tile([P, T], U8, name="x_planes", align_bytes=ALIGN)
+        x_head = [keep.tile([P, HEAD], U32, name="x_head%d" % z, align_bytes=ALIGN) for z in range(PASSES)]
+        x_rest = [keep.tile([P, T - HEAD], U32, name="x_rest%d" % z, align_bytes=ALIGN) for z in range(PASSES)]
+        w_raw = stage.tile([P, PASSES, PACK, N], F32, name="w_raw", offset=2 * T, align_bytes=ALIGN)
+        w_grouped = [keep.tile([P, N, PACK], BF16, name="w_grouped%d" % z, align_bytes=ALIGN) for z in range(PASSES)]
+        w_codes = [keep.tile([P, N], U32, name="w_codes%d" % z, align_bytes=ALIGN) for z in range(PASSES)]
+        w_scales = [keep.tile([P, N], U8, name="w_scales%d" % z, align_bytes=ALIGN) for z in range(PASSES)]
+        add_head = keep.tile([P, HEAD], F32, name="add_head", align_bytes=ALIGN)
+        add_rest = keep.tile([P, T - HEAD], F32, name="add_rest", align_bytes=ALIGN)
         y = [psum.tile([P, PIECE], F32, name="y%d" % i) for i in range(T // PIECE)]
 
         nc.vector.memset(x_planes[:].bitcast(I32), 0)
@@ -96,11 +97,11 @@ def tile_picked_widxput_add_l_kernel(tc, x_words, x_scales, mem, w1, slot, out):
             for i in range(1, T // PIECE):
                 project(i, z, x_rest[z][:, (i - 1) * PIECE : i * PIECE])
 
-        store = stage.tile([P, U], F32, name="store", offset=4 * T)
+        store = stage.tile([P, U], F32, name="store", offset=4 * T, align_bytes=ALIGN)
         nc.vector.tensor_copy(store[:, SCALAR_COPY:], table[:, SCALAR_COPY:])
         nc.scalar.copy(store[:, :SCALAR_COPY], table[:, :SCALAR_COPY])
-        old_head = stage.tile([P, HEAD], F32, name="old_head", offset=4 * (T - HEAD))
-        old_rest = stage.tile([P, T - HEAD], F32, name="old_rest", offset=0)
+        old_head = stage.tile([P, HEAD], F32, name="old_head", offset=4 * (T - HEAD), align_bytes=ALIGN)
+        old_rest = stage.tile([P, T - HEAD], F32, name="old_rest", offset=0, align_bytes=ALIGN)
         nc.vector.tensor_copy(old_head[:], looked_up(0, HEAD))
         nc.vector.tensor_copy(old_rest[:], looked_up(HEAD, T - HEAD))
         nc.scalar.copy(add_head[:], y[0][:])

@@ -19,8 +19,8 @@ PACK = 4
 PASSES = K // (P * PACK)
 PIECE = 128
 HEAD = 128
-SCALAR_COPY = 832
-VECTOR_CAST = 96
+SCALAR_COPY = 880
+VECTOR_CAST = 80
 LINE = 4
 ALIGN = 256
 

@@ -13,14 +13,17 @@ U16 = mybir.dt.uint16
 U8 = mybir.dt.uint8
 FP8X4 = mybir.dt.float8_e4m3fn_x4
 ADD = mybir.AluOpType.add
+MULT = mybir.AluOpType.mult
+COPY = mybir.ActivationFunctionType.Copy
 
 P = 128
 PACK = 4
 PASSES = K // (P * PACK)
 PIECE = 128
-HEAD = 128
-SCALAR_COPY = 880
-VECTOR_CAST = 80
+X_LOADS = ((0, 128), (128, 256), (256, 512))
+SCALAR_END = 320
+SCALAR_FILL = 256
+STORES = 4
 LINE = 4
 ALIGN = 256
 
@@ -34,21 +37,34 @@ def tile_picked_widxput_add_l_kernel(tc, x_words, x_scales, mem, w1, slot, out):
 
         offsets = keep.tile([P, T // 16], U16, name="offsets", align_bytes=ALIGN)
         table = keep.tile([P, U], F32, name="table", align_bytes=ALIGN)
+        mask = keep.tile([P, U], F32, name="mask", align_bytes=ALIGN)
+        zeros = keep.tile([P, SCALAR_FILL], F32, name="zeros", align_bytes=ALIGN)
+        fresh = keep.tile([P, U], F32, name="fresh", align_bytes=ALIGN)
         x_planes = keep.tile([P, T], U8, name="x_planes", align_bytes=ALIGN)
-        x_head = [keep.tile([P, HEAD], U32, name="x_head%d" % z, align_bytes=ALIGN) for z in range(PASSES)]
-        x_rest = [keep.tile([P, T - HEAD], U32, name="x_rest%d" % z, align_bytes=ALIGN) for z in range(PASSES)]
-        w_raw = stage.tile([P, PASSES, PACK, N], F32, name="w_raw", offset=2 * T, align_bytes=ALIGN)
-        w_grouped = [keep.tile([P, N, PACK], BF16, name="w_grouped%d" % z, align_bytes=ALIGN) for z in range(PASSES)]
+        x_part = [
+            keep.tile([P, PASSES, end - first], U32, name="x_part%d" % first, align_bytes=ALIGN) for first, end in X_LOADS
+        ]
+        w_raw = keep.tile([P, PASSES, PACK, N], F32, name="w_raw", align_bytes=ALIGN)
+        w_grouped = [
+            stage.tile([P, N, PACK], BF16, name="w_grouped%d" % z, offset=2 * N * PACK * z, align_bytes=ALIGN)
+            for z in range(PASSES)
+        ]
         w_codes = [keep.tile([P, N], U32, name="w_codes%d" % z, align_bytes=ALIGN) for z in range(PASSES)]
         w_scales = [keep.tile([P, N], U8, name="w_scales%d" % z, align_bytes=ALIGN) for z in range(PASSES)]
-        add_head = keep.tile([P, HEAD], F32, name="add_head", align_bytes=ALIGN)
-        add_rest = keep.tile([P, T - HEAD], F32, name="add_rest", align_bytes=ALIGN)
+        old = keep.tile([P, T], F32, name="old", align_bytes=ALIGN)
+        new = keep.tile([P, T], F32, name="new", align_bytes=ALIGN)
         y = [psum.tile([P, PIECE], F32, name="y%d" % i) for i in range(T // PIECE)]
 
+        def slots(first, end):
+            return offsets[:, first // 16 : end // 16]
+
         nc.vector.memset(x_planes[:].bitcast(I32), 0)
+        nc.vector.memset(zeros[:], 0.0)
+        nc.vector.memset(mask[:, SCALAR_FILL:], 1.0)
+        nc.scalar.activation(mask[:, :SCALAR_FILL], zeros[:], COPY, bias=1.0)
+        nc.gpsimd.memset(fresh[:], 0.0)
 
         x_rows = x_words.rearrange("z p c r -> p z (c r)")
-        nc.sync.dma_start(out=x_head[0][:].bitcast(I32), in_=x_rows[:, 0, : PACK * HEAD].bitcast(I32))
         nc.sync.dma_start(offsets[:], slot)
         nc.sync.dma_start(out=w_raw[:], in_=w1.rearrange("(z p j) m -> p z j m", p=P, j=PACK))
         nc.sync.dma_start(out=table[:], in_=mem)
@@ -57,16 +73,16 @@ def tile_picked_widxput_add_l_kernel(tc, x_words, x_scales, mem, w1, slot, out):
                 out=x_planes[32 * q : 32 * q + 4 * PASSES, :].bitcast(I32),
                 in_=x_scales[:, 4 * q : 4 * q + 4, :].bitcast(I32),
             )
-        nc.sync.dma_start(out=x_head[1][:].bitcast(I32), in_=x_rows[:, 1, : PACK * HEAD].bitcast(I32))
-        for z in range(PASSES):
-            nc.sync.dma_start(out=x_rest[z][:].bitcast(I32), in_=x_rows[:, z, PACK * HEAD :].bitcast(I32))
+        for part, (first, end) in zip(x_part, X_LOADS):
+            nc.sync.dma_start(out=part[:].bitcast(I32), in_=x_rows[:, :, PACK * first : PACK * end].bitcast(I32))
+
+        nc.scalar.activation(mask[:].indirect(slots(PIECE, SCALAR_END)), zeros[:, : SCALAR_END - PIECE], COPY)
 
         for z in range(PASSES):
-            for copy, cols in ((nc.vector.tensor_copy, slice(0, VECTOR_CAST)), (nc.scalar.copy, slice(VECTOR_CAST, N))):
-                copy(
-                    out=w_grouped[z][:, cols].rearrange("p (c i) j -> p c j i", i=LINE),
-                    in_=w_raw[:, z, :, cols].rearrange("p j (c i) -> p c j i", i=LINE),
-                )
+            nc.vector.tensor_copy(
+                out=w_grouped[z][:].rearrange("p (c i) j -> p c j i", i=LINE),
+                in_=w_raw[:, z].rearrange("p j (c i) -> p c j i", i=LINE),
+            )
         for z in range(PASSES):
             nc.vector.quantize_mx(
                 out=w_codes[z][:].bitcast(FP8X4),
@@ -74,39 +90,30 @@ def tile_picked_widxput_add_l_kernel(tc, x_words, x_scales, mem, w1, slot, out):
                 in_=w_grouped[z][:].rearrange("p m j -> p (m j)"),
             )
 
-        def project(piece, z, words):
-            nc.tensor.matmul_mx(
-                out=y[piece][:],
-                lhsT=w_codes[z][:].bitcast(FP8X4),
-                lhsT_scale=w_scales[z][:],
-                rhs=words.bitcast(FP8X4),
-                rhs_scale=x_planes[4 * z :, piece * PIECE : (piece + 1) * PIECE],
-                start=(z == 0),
-                stop=(z == PASSES - 1),
-            )
+        for part, (first, end) in zip(x_part, X_LOADS):
+            for col in range(first, end, PIECE):
+                for z in range(PASSES):
+                    nc.tensor.matmul_mx(
+                        out=y[col // PIECE][:],
+                        lhsT=w_codes[z][:].bitcast(FP8X4),
+                        lhsT_scale=w_scales[z][:],
+                        rhs=part[:, z, col - first : col - first + PIECE].bitcast(FP8X4),
+                        rhs_scale=x_planes[4 * z :, col : col + PIECE],
+                        start=(z == 0),
+                        stop=(z == PASSES - 1),
+                    )
 
-        def listed(first, count):
-            return store[:].indirect(offsets[:, first // 16 : (first + count) // 16])
-
-        def looked_up(first, count):
-            return table[:].indirect(offsets[:, first // 16 : (first + count) // 16])
-
-        for z in range(PASSES):
-            project(0, z, x_head[z][:])
-        for z in range(PASSES):
-            for i in range(1, T // PIECE):
-                project(i, z, x_rest[z][:, (i - 1) * PIECE : i * PIECE])
-
-        store = stage.tile([P, U], F32, name="store", offset=4 * T, align_bytes=ALIGN)
-        nc.vector.tensor_copy(store[:, SCALAR_COPY:], table[:, SCALAR_COPY:])
-        nc.scalar.copy(store[:, :SCALAR_COPY], table[:, :SCALAR_COPY])
-        old_head = stage.tile([P, HEAD], F32, name="old_head", offset=4 * (T - HEAD), align_bytes=ALIGN)
-        old_rest = stage.tile([P, T - HEAD], F32, name="old_rest", offset=0, align_bytes=ALIGN)
-        nc.vector.tensor_copy(old_head[:], looked_up(0, HEAD))
-        nc.vector.tensor_copy(old_rest[:], looked_up(HEAD, T - HEAD))
-        nc.scalar.copy(add_head[:], y[0][:])
-        for i in range(1, T // PIECE):
-            nc.scalar.copy(add_rest[:, (i - 1) * PIECE : i * PIECE], y[i][:])
-        nc.vector.tensor_tensor(listed(0, HEAD), old_head[:], add_head[:], ADD)
-        nc.vector.tensor_tensor(listed(HEAD, T - HEAD), old_rest[:], add_rest[:], ADD)
-        nc.sync.dma_start(out=out, in_=store[:])
+        kept = stage.tile([P, U], F32, name="kept", offset=0, align_bytes=ALIGN)
+        nc.vector.tensor_tensor(kept[:], table[:], mask[:], MULT)
+        nc.scalar.activation(old[:, :PIECE], table[:].indirect(slots(0, PIECE)), COPY)
+        nc.scalar.activation(old[:, PIECE:], table[:].indirect(slots(PIECE, T)), COPY)
+        for i in range(T // PIECE):
+            cols = slice(i * PIECE, (i + 1) * PIECE)
+            nc.vector.tensor_tensor(new[:, cols], old[:, cols], y[i][:], ADD)
+        nc.scalar.activation(kept[:].indirect(slots(0, PIECE)), new[:, :PIECE], COPY)
+        nc.scalar.activation(fresh[:].indirect(slots(PIECE, SCALAR_END)), new[:, PIECE:SCALAR_END], COPY)
+        nc.vector.tensor_copy(kept[:].indirect(slots(SCALAR_END, T)), new[:, SCALAR_END:])
+        for i in range(STORES):
+            cols = slice(i * U // STORES, (i + 1) * U // STORES)
+            nc.vector.tensor_tensor(mask[:, cols], fresh[:, cols], kept[:, cols], ADD)
+            nc.sync.dma_start(out=out[:, cols], in_=mask[:, cols])

@@ -20,8 +20,8 @@ P = 128
 PACK = 4
 PASSES = K // (P * PACK)
 PIECE = 128
-X_LOADS = ((0, 128), (128, 256), (256, 512))
-SCALAR_END = 320
+REST_ORDER = (2, 3, 1)
+SCALAR_END = 288
 SCALAR_FILL = 256
 STORES = 4
 LINE = 4
@@ -41,9 +41,8 @@ def tile_picked_widxput_add_l_kernel(tc, x_words, x_scales, mem, w1, slot, out):
         zeros = keep.tile([P, SCALAR_FILL], F32, name="zeros", align_bytes=ALIGN)
         fresh = keep.tile([P, U], F32, name="fresh", align_bytes=ALIGN)
         x_planes = keep.tile([P, T], U8, name="x_planes", align_bytes=ALIGN)
-        x_part = [
-            keep.tile([P, PASSES, end - first], U32, name="x_part%d" % first, align_bytes=ALIGN) for first, end in X_LOADS
-        ]
+        x_head = keep.tile([P, PASSES, PIECE], U32, name="x_head", align_bytes=ALIGN)
+        x_rest = [keep.tile([P, T - PIECE], U32, name="x_rest%d" % z, align_bytes=ALIGN) for z in range(PASSES)]
         w_raw = keep.tile([P, PASSES, PACK, N], F32, name="w_raw", align_bytes=ALIGN)
         w_grouped = [
             stage.tile([P, N, PACK], BF16, name="w_grouped%d" % z, offset=2 * N * PACK * z, align_bytes=ALIGN)
@@ -58,7 +57,6 @@ def tile_picked_widxput_add_l_kernel(tc, x_words, x_scales, mem, w1, slot, out):
         def slots(first, end):
             return offsets[:, first // 16 : end // 16]
 
-        nc.vector.memset(x_planes[:].bitcast(I32), 0)
         nc.vector.memset(zeros[:], 0.0)
         nc.vector.memset(mask[:, SCALAR_FILL:], 1.0)
         nc.scalar.activation(mask[:, :SCALAR_FILL], zeros[:], COPY, bias=1.0)
@@ -73,10 +71,11 @@ def tile_picked_widxput_add_l_kernel(tc, x_words, x_scales, mem, w1, slot, out):
                 out=x_planes[32 * q : 32 * q + 4 * PASSES, :].bitcast(I32),
                 in_=x_scales[:, 4 * q : 4 * q + 4, :].bitcast(I32),
             )
-        for part, (first, end) in zip(x_part, X_LOADS):
-            nc.sync.dma_start(out=part[:].bitcast(I32), in_=x_rows[:, :, PACK * first : PACK * end].bitcast(I32))
+        nc.sync.dma_start(out=x_head[:].bitcast(I32), in_=x_rows[:, :, : PACK * PIECE].bitcast(I32))
+        for z in range(PASSES):
+            nc.sync.dma_start(out=x_rest[z][:].bitcast(I32), in_=x_rows[:, z, PACK * PIECE :].bitcast(I32))
 
-        nc.scalar.activation(mask[:].indirect(slots(PIECE, SCALAR_END)), zeros[:, : SCALAR_END - PIECE], COPY)
+        nc.scalar.activation(mask[:].indirect(slots(SCALAR_END, T)), zeros[:, : T - SCALAR_END], COPY)
 
         for z in range(PASSES):
             nc.vector.tensor_copy(
@@ -90,29 +89,33 @@ def tile_picked_widxput_add_l_kernel(tc, x_words, x_scales, mem, w1, slot, out):
                 in_=w_grouped[z][:].rearrange("p m j -> p (m j)"),
             )
 
-        for part, (first, end) in zip(x_part, X_LOADS):
-            for col in range(first, end, PIECE):
-                for z in range(PASSES):
-                    nc.tensor.matmul_mx(
-                        out=y[col // PIECE][:],
-                        lhsT=w_codes[z][:].bitcast(FP8X4),
-                        lhsT_scale=w_scales[z][:],
-                        rhs=part[:, z, col - first : col - first + PIECE].bitcast(FP8X4),
-                        rhs_scale=x_planes[4 * z :, col : col + PIECE],
-                        start=(z == 0),
-                        stop=(z == PASSES - 1),
-                    )
+        def project(piece, z, words):
+            nc.tensor.matmul_mx(
+                out=y[piece][:],
+                lhsT=w_codes[z][:].bitcast(FP8X4),
+                lhsT_scale=w_scales[z][:],
+                rhs=words.bitcast(FP8X4),
+                rhs_scale=x_planes[4 * z :, piece * PIECE : (piece + 1) * PIECE],
+                start=(z == 0),
+                stop=(z == PASSES - 1),
+            )
+
+        for z in range(PASSES):
+            project(0, z, x_head[:, z])
+        for z in range(PASSES):
+            for i in REST_ORDER:
+                project(i, z, x_rest[z][:, (i - 1) * PIECE : i * PIECE])
 
         kept = stage.tile([P, U], F32, name="kept", offset=0, align_bytes=ALIGN)
         nc.vector.tensor_tensor(kept[:], table[:], mask[:], MULT)
         nc.scalar.activation(old[:, :PIECE], table[:].indirect(slots(0, PIECE)), COPY)
         nc.scalar.activation(old[:, PIECE:], table[:].indirect(slots(PIECE, T)), COPY)
-        for i in range(T // PIECE):
+        for i in (0,) + REST_ORDER:
             cols = slice(i * PIECE, (i + 1) * PIECE)
             nc.vector.tensor_tensor(new[:, cols], old[:, cols], y[i][:], ADD)
         nc.scalar.activation(kept[:].indirect(slots(0, PIECE)), new[:, :PIECE], COPY)
-        nc.scalar.activation(fresh[:].indirect(slots(PIECE, SCALAR_END)), new[:, PIECE:SCALAR_END], COPY)
-        nc.vector.tensor_copy(kept[:].indirect(slots(SCALAR_END, T)), new[:, SCALAR_END:])
+        nc.scalar.activation(kept[:].indirect(slots(PIECE, SCALAR_END)), new[:, PIECE:SCALAR_END], COPY)
+        nc.vector.tensor_copy(fresh[:].indirect(slots(SCALAR_END, T)), new[:, SCALAR_END:])
         for i in range(STORES):
             cols = slice(i * U // STORES, (i + 1) * U // STORES)
             nc.vector.tensor_tensor(mask[:, cols], fresh[:, cols], kept[:, cols], ADD)

@@ -41,7 +41,7 @@ def tile_picked_widxput_add_l_kernel(tc, x_words, x_scales, mem, w1, slot, out):
         zeros = keep.tile([P, SCALAR_FILL], F32, name="zeros", align_bytes=ALIGN)
         fresh = keep.tile([P, U], F32, name="fresh", align_bytes=ALIGN)
         x_planes = keep.tile([P, T], U8, name="x_planes", align_bytes=ALIGN)
-        x_head = keep.tile([P, PASSES, PIECE], U32, name="x_head", align_bytes=ALIGN)
+        x_head = [keep.tile([P, PIECE], U32, name="x_head%d" % z, align_bytes=ALIGN) for z in range(PASSES)]
         x_rest = [keep.tile([P, T - PIECE], U32, name="x_rest%d" % z, align_bytes=ALIGN) for z in range(PASSES)]
         w_raw = keep.tile([P, PASSES, PACK, N], F32, name="w_raw", align_bytes=ALIGN)
         w_grouped = [
@@ -63,6 +63,7 @@ def tile_picked_widxput_add_l_kernel(tc, x_words, x_scales, mem, w1, slot, out):
         nc.gpsimd.memset(fresh[:], 0.0)
 
         x_rows = x_words.rearrange("z p c r -> p z (c r)")
+        nc.sync.dma_start(out=x_head[0][:].bitcast(I32), in_=x_rows[:, 0, : PACK * PIECE].bitcast(I32))
         nc.sync.dma_start(offsets[:], slot)
         nc.sync.dma_start(out=w_raw[:], in_=w1.rearrange("(z p j) m -> p z j m", p=P, j=PACK))
         nc.sync.dma_start(out=table[:], in_=mem)
@@ -71,7 +72,7 @@ def tile_picked_widxput_add_l_kernel(tc, x_words, x_scales, mem, w1, slot, out):
                 out=x_planes[32 * q : 32 * q + 4 * PASSES, :].bitcast(I32),
                 in_=x_scales[:, 4 * q : 4 * q + 4, :].bitcast(I32),
             )
-        nc.sync.dma_start(out=x_head[:].bitcast(I32), in_=x_rows[:, :, : PACK * PIECE].bitcast(I32))
+        nc.sync.dma_start(out=x_head[1][:].bitcast(I32), in_=x_rows[:, 1, : PACK * PIECE].bitcast(I32))
         for z in range(PASSES):
             nc.sync.dma_start(out=x_rest[z][:].bitcast(I32), in_=x_rows[:, z, PACK * PIECE :].bitcast(I32))
 
@@ -101,7 +102,7 @@ def tile_picked_widxput_add_l_kernel(tc, x_words, x_scales, mem, w1, slot, out):
             )
 
         for z in range(PASSES):
-            project(0, z, x_head[:, z])
+            project(0, z, x_head[z][:])
         for z in range(PASSES):
             for i in REST_ORDER:
                 project(i, z, x_rest[z][:, (i - 1) * PIECE : i * PIECE])

@@ -32,22 +32,19 @@ def tile_picked_widxput_add_l_kernel(tc, x_words, x_scales, mem, w1, slot, out):
     nc = tc.nc
     with ExitStack() as ctx:
         keep = ctx.enter_context(tc.tile_pool(name="keep", bufs=1))
-        stage = ctx.enter_context(tc.tile_pool(name="stage", bufs=1))
         psum = ctx.enter_context(tc.psum_pool(name="psum", bufs=1))
 
         offsets = keep.tile([P, T // 16], U16, name="offsets", align_bytes=ALIGN)
         table = keep.tile([P, U], F32, name="table", align_bytes=ALIGN)
         mask = keep.tile([P, U], F32, name="mask", align_bytes=ALIGN)
         zeros = keep.tile([P, SCALAR_FILL], F32, name="zeros", align_bytes=ALIGN)
+        kept = keep.tile([P, U], F32, name="kept", align_bytes=ALIGN)
         fresh = keep.tile([P, U], F32, name="fresh", align_bytes=ALIGN)
         x_planes = keep.tile([P, T], U8, name="x_planes", align_bytes=ALIGN)
         x_head = [keep.tile([P, PIECE], U32, name="x_head%d" % z, align_bytes=ALIGN) for z in range(PASSES)]
         x_rest = [keep.tile([P, T - PIECE], U32, name="x_rest%d" % z, align_bytes=ALIGN) for z in range(PASSES)]
         w_raw = keep.tile([P, PASSES, PACK, N], F32, name="w_raw", align_bytes=ALIGN)
-        w_grouped = [
-            stage.tile([P, N, PACK], BF16, name="w_grouped%d" % z, offset=2 * N * PACK * z, align_bytes=ALIGN)
-            for z in range(PASSES)
-        ]
+        w_grouped = [keep.tile([P, N, PACK], BF16, name="w_grouped%d" % z, align_bytes=ALIGN) for z in range(PASSES)]
         w_codes = [keep.tile([P, N], U32, name="w_codes%d" % z, align_bytes=ALIGN) for z in range(PASSES)]
         w_scales = [keep.tile([P, N], U8, name="w_scales%d" % z, align_bytes=ALIGN) for z in range(PASSES)]
         old = keep.tile([P, T], F32, name="old", align_bytes=ALIGN)
@@ -60,7 +57,7 @@ def tile_picked_widxput_add_l_kernel(tc, x_words, x_scales, mem, w1, slot, out):
         nc.vector.memset(zeros[:], 0.0)
         nc.vector.memset(mask[:, SCALAR_FILL:], 1.0)
         nc.scalar.activation(mask[:, :SCALAR_FILL], zeros[:], COPY, bias=1.0)
-        nc.gpsimd.memset(fresh[:], 0.0)
+        nc.vector.memset(fresh[:], 0.0)
 
         x_rows = x_words.rearrange("z p c r -> p z (c r)")
         nc.sync.dma_start(out=x_head[0][:].bitcast(I32), in_=x_rows[:, 0, : PACK * PIECE].bitcast(I32))
@@ -107,7 +104,6 @@ def tile_picked_widxput_add_l_kernel(tc, x_words, x_scales, mem, w1, slot, out):
             for i in REST_ORDER:
                 project(i, z, x_rest[z][:, (i - 1) * PIECE : i * PIECE])
 
-        kept = stage.tile([P, U], F32, name="kept", offset=0, align_bytes=ALIGN)
         nc.vector.tensor_tensor(kept[:], table[:], mask[:], MULT)
         nc.scalar.activation(old[:, :PIECE], table[:].indirect(slots(0, PIECE)), COPY)
         nc.scalar.activation(old[:, PIECE:], table[:].indirect(slots(PIECE, T)), COPY)

@@ -20,8 +20,7 @@ P = 128
 PACK = 4
 PASSES = K // (P * PACK)
 PIECE = 128
-REST_ORDER = (2, 3, 1)
-SCALAR_END = 288
+VECTOR_END = 352
 SCALAR_FILL = 256
 STORES = 4
 LINE = 4
@@ -41,8 +40,9 @@ def tile_picked_widxput_add_l_kernel(tc, x_words, x_scales, mem, w1, slot, out):
         kept = keep.tile([P, U], F32, name="kept", align_bytes=ALIGN)
         fresh = keep.tile([P, U], F32, name="fresh", align_bytes=ALIGN)
         x_planes = keep.tile([P, T], U8, name="x_planes", align_bytes=ALIGN)
-        x_head = [keep.tile([P, PIECE], U32, name="x_head%d" % z, align_bytes=ALIGN) for z in range(PASSES)]
-        x_rest = [keep.tile([P, T - PIECE], U32, name="x_rest%d" % z, align_bytes=ALIGN) for z in range(PASSES)]
+        cuts = (PIECE, 2 * PIECE)
+        x_early = [keep.tile([P, cuts[z]], U32, name="x_early%d" % z, align_bytes=ALIGN) for z in range(PASSES)]
+        x_late = [keep.tile([P, T - cuts[z]], U32, name="x_late%d" % z, align_bytes=ALIGN) for z in range(PASSES)]
         w_raw = keep.tile([P, PASSES, PACK, N], F32, name="w_raw", align_bytes=ALIGN)
         w_grouped = [keep.tile([P, N, PACK], BF16, name="w_grouped%d" % z, align_bytes=ALIGN) for z in range(PASSES)]
         w_codes = [keep.tile([P, N], U32, name="w_codes%d" % z, align_bytes=ALIGN) for z in range(PASSES)]
@@ -60,7 +60,7 @@ def tile_picked_widxput_add_l_kernel(tc, x_words, x_scales, mem, w1, slot, out):
         nc.vector.memset(fresh[:], 0.0)
 
         x_rows = x_words.rearrange("z p c r -> p z (c r)")
-        nc.sync.dma_start(out=x_head[0][:].bitcast(I32), in_=x_rows[:, 0, : PACK * PIECE].bitcast(I32))
+        nc.sync.dma_start(out=x_early[0][:].bitcast(I32), in_=x_rows[:, 0, : PACK * cuts[0]].bitcast(I32))
         nc.sync.dma_start(offsets[:], slot)
         nc.sync.dma_start(out=w_raw[:], in_=w1.rearrange("(z p j) m -> p z j m", p=P, j=PACK))
         nc.sync.dma_start(out=table[:], in_=mem)
@@ -69,11 +69,11 @@ def tile_picked_widxput_add_l_kernel(tc, x_words, x_scales, mem, w1, slot, out):
                 out=x_planes[32 * q : 32 * q + 4 * PASSES, :].bitcast(I32),
                 in_=x_scales[:, 4 * q : 4 * q + 4, :].bitcast(I32),
             )
-        nc.sync.dma_start(out=x_head[1][:].bitcast(I32), in_=x_rows[:, 1, : PACK * PIECE].bitcast(I32))
+        nc.sync.dma_start(out=x_early[1][:].bitcast(I32), in_=x_rows[:, 1, : PACK * cuts[1]].bitcast(I32))
         for z in range(PASSES):
-            nc.sync.dma_start(out=x_rest[z][:].bitcast(I32), in_=x_rows[:, z, PACK * PIECE :].bitcast(I32))
+            nc.sync.dma_start(out=x_late[z][:].bitcast(I32), in_=x_rows[:, z, PACK * cuts[z] :].bitcast(I32))
 
-        nc.scalar.activation(mask[:].indirect(slots(SCALAR_END, T)), zeros[:, : T - SCALAR_END], COPY)
+        nc.scalar.activation(mask[:].indirect(slots(PIECE, VECTOR_END)), zeros[:, : VECTOR_END - PIECE], COPY)
 
         for z in range(PASSES):
             nc.vector.tensor_copy(
@@ -87,32 +87,36 @@ def tile_picked_widxput_add_l_kernel(tc, x_words, x_scales, mem, w1, slot, out):
                 in_=w_grouped[z][:].rearrange("p m j -> p (m j)"),
             )
 
-        def project(piece, z, words):
+        def project(piece, z, first):
+            col = piece * PIECE
+            words = x_early[z][:, col : col + PIECE] if col < cuts[z] else x_late[z][:, col - cuts[z] : col - cuts[z] + PIECE]
             nc.tensor.matmul_mx(
                 out=y[piece][:],
                 lhsT=w_codes[z][:].bitcast(FP8X4),
                 lhsT_scale=w_scales[z][:],
                 rhs=words.bitcast(FP8X4),
-                rhs_scale=x_planes[4 * z :, piece * PIECE : (piece + 1) * PIECE],
-                start=(z == 0),
-                stop=(z == PASSES - 1),
+                rhs_scale=x_planes[4 * z :, col : col + PIECE],
+                start=first,
+                stop=not first,
             )
 
+        project(0, 0, True)
+        project(0, 1, False)
+        project(1, 1, True)
+        project(1, 0, False)
         for z in range(PASSES):
-            project(0, z, x_head[z][:])
-        for z in range(PASSES):
-            for i in REST_ORDER:
-                project(i, z, x_rest[z][:, (i - 1) * PIECE : i * PIECE])
+            for i in (2, 3):
+                project(i, z, z == 0)
 
         nc.vector.tensor_tensor(kept[:], table[:], mask[:], MULT)
         nc.scalar.activation(old[:, :PIECE], table[:].indirect(slots(0, PIECE)), COPY)
         nc.scalar.activation(old[:, PIECE:], table[:].indirect(slots(PIECE, T)), COPY)
-        for i in (0,) + REST_ORDER:
+        for i in range(T // PIECE):
             cols = slice(i * PIECE, (i + 1) * PIECE)
             nc.vector.tensor_tensor(new[:, cols], old[:, cols], y[i][:], ADD)
         nc.scalar.activation(kept[:].indirect(slots(0, PIECE)), new[:, :PIECE], COPY)
-        nc.scalar.activation(kept[:].indirect(slots(PIECE, SCALAR_END)), new[:, PIECE:SCALAR_END], COPY)
-        nc.vector.tensor_copy(fresh[:].indirect(slots(SCALAR_END, T)), new[:, SCALAR_END:])
+        nc.scalar.activation(kept[:].indirect(slots(VECTOR_END, T)), new[:, VECTOR_END:], COPY)
+        nc.vector.tensor_copy(fresh[:].indirect(slots(PIECE, VECTOR_END)), new[:, PIECE:VECTOR_END])
         for i in range(STORES):
             cols = slice(i * U // STORES, (i + 1) * U // STORES)
             nc.vector.tensor_tensor(mask[:, cols], fresh[:, cols], kept[:, cols], ADD)

from contextlib import ExitStack

import concourse.mybir as mybir

K, T, N, U = 1024, 512, 128, 1024
FLOPS = 2 * K * T * N

F32 = mybir.dt.float32
BF16 = mybir.dt.bfloat16
I32 = mybir.dt.int32
U32 = mybir.dt.uint32
U16 = mybir.dt.uint16
U8 = mybir.dt.uint8
FP8X4 = mybir.dt.float8_e4m3fn_x4
ADD = mybir.AluOpType.add
MULT = mybir.AluOpType.mult
COPY = mybir.ActivationFunctionType.Copy

P = 128
PACK = 4
PASSES = K // (P * PACK)
PIECE = 128
VECTOR_END = 352
SCALAR_FILL = 256
STORES = 4
LINE = 4
ALIGN = 256


def tile_picked_widxput_add_l_kernel(tc, x_words, x_scales, mem, w1, slot, out):
    nc = tc.nc
    with ExitStack() as ctx:
        keep = ctx.enter_context(tc.tile_pool(name="keep", bufs=1))
        psum = ctx.enter_context(tc.psum_pool(name="psum", bufs=1))

        offsets = keep.tile([P, T // 16], U16, name="offsets", align_bytes=ALIGN)
        table = keep.tile([P, U], F32, name="table", align_bytes=ALIGN)
        mask = keep.tile([P, U], F32, name="mask", align_bytes=ALIGN)
        zeros = keep.tile([P, SCALAR_FILL], F32, name="zeros", align_bytes=ALIGN)
        kept = keep.tile([P, U], F32, name="kept", align_bytes=ALIGN)
        fresh = keep.tile([P, U], F32, name="fresh", align_bytes=ALIGN)
        x_planes = keep.tile([P, T], U8, name="x_planes", align_bytes=ALIGN)
        cuts = (PIECE, 2 * PIECE)
        x_early = [keep.tile([P, cuts[z]], U32, name="x_early%d" % z, align_bytes=ALIGN) for z in range(PASSES)]
        x_late = [keep.tile([P, T - cuts[z]], U32, name="x_late%d" % z, align_bytes=ALIGN) for z in range(PASSES)]
        w_raw = keep.tile([P, PASSES, PACK, N], F32, name="w_raw", align_bytes=ALIGN)
        w_grouped = [keep.tile([P, N, PACK], BF16, name="w_grouped%d" % z, align_bytes=ALIGN) for z in range(PASSES)]
        w_codes = [keep.tile([P, N], U32, name="w_codes%d" % z, align_bytes=ALIGN) for z in range(PASSES)]
        w_scales = [keep.tile([P, N], U8, name="w_scales%d" % z, align_bytes=ALIGN) for z in range(PASSES)]
        old = keep.tile([P, T], F32, name="old", align_bytes=ALIGN)
        new = keep.tile([P, T], F32, name="new", align_bytes=ALIGN)
        y = [psum.tile([P, PIECE], F32, name="y%d" % i) for i in range(T // PIECE)]

        def slots(first, end):
            return offsets[:, first // 16 : end // 16]

        nc.vector.memset(zeros[:], 0.0)
        nc.vector.memset(mask[:, SCALAR_FILL:], 1.0)
        nc.scalar.activation(mask[:, :SCALAR_FILL], zeros[:], COPY, bias=1.0)
        nc.vector.memset(fresh[:], 0.0)

        x_rows = x_words.rearrange("z p c r -> p z (c r)")
        nc.sync.dma_start(out=x_early[0][:].bitcast(I32), in_=x_rows[:, 0, : PACK * cuts[0]].bitcast(I32))
        nc.sync.dma_start(offsets[:], slot)
        nc.sync.dma_start(out=w_raw[:], in_=w1.rearrange("(z p j) m -> p z j m", p=P, j=PACK))
        nc.sync.dma_start(out=table[:], in_=mem)
        for q in range(4):
            nc.sync.dma_start(
                out=x_planes[32 * q : 32 * q + 4 * PASSES, :].bitcast(I32),
                in_=x_scales[:, 4 * q : 4 * q + 4, :].bitcast(I32),
            )
        nc.sync.dma_start(out=x_early[1][:].bitcast(I32), in_=x_rows[:, 1, : PACK * cuts[1]].bitcast(I32))
        for z in range(PASSES):
            nc.sync.dma_start(out=x_late[z][:].bitcast(I32), in_=x_rows[:, z, PACK * cuts[z] :].bitcast(I32))

        nc.scalar.activation(mask[:].indirect(slots(PIECE, VECTOR_END)), zeros[:, : VECTOR_END - PIECE], COPY)

        for z in range(PASSES):
            nc.vector.tensor_copy(
                out=w_grouped[z][:].rearrange("p (c i) j -> p c j i", i=LINE),
                in_=w_raw[:, z].rearrange("p j (c i) -> p c j i", i=LINE),
            )
        for z in range(PASSES):
            nc.vector.quantize_mx(
                out=w_codes[z][:].bitcast(FP8X4),
                scales=w_scales[z][:],
                in_=w_grouped[z][:].rearrange("p m j -> p (m j)"),
            )

        def project(piece, z, first):
            col = piece * PIECE
            words = x_early[z][:, col : col + PIECE] if col < cuts[z] else x_late[z][:, col - cuts[z] : col - cuts[z] + PIECE]
            nc.tensor.matmul_mx(
                out=y[piece][:],
                lhsT=w_codes[z][:].bitcast(FP8X4),
                lhsT_scale=w_scales[z][:],
                rhs=words.bitcast(FP8X4),
                rhs_scale=x_planes[4 * z :, col : col + PIECE],
                start=first,
                stop=not first,
            )

        project(0, 0, True)
        project(0, 1, False)
        project(1, 1, True)
        project(1, 0, False)
        for z in range(PASSES):
            for i in (2, 3):
                project(i, z, z == 0)

        nc.vector.tensor_tensor(kept[:], table[:], mask[:], MULT)
        nc.scalar.activation(old[:, :PIECE], table[:].indirect(slots(0, PIECE)), COPY)
        nc.scalar.activation(old[:, PIECE:], table[:].indirect(slots(PIECE, T)), COPY)
        for i in range(T // PIECE):
            cols = slice(i * PIECE, (i + 1) * PIECE)
            nc.vector.tensor_tensor(new[:, cols], old[:, cols], y[i][:], ADD)
        nc.scalar.activation(kept[:].indirect(slots(0, PIECE)), new[:, :PIECE], COPY)
        nc.scalar.activation(kept[:].indirect(slots(VECTOR_END, T)), new[:, VECTOR_END:], COPY)
        nc.vector.tensor_copy(fresh[:].indirect(slots(PIECE, VECTOR_END)), new[:, PIECE:VECTOR_END])
        for i in range(STORES):
            cols = slice(i * U // STORES, (i + 1) * U // STORES)
            nc.vector.tensor_tensor(mask[:, cols], fresh[:, cols], kept[:, cols], ADD)
            nc.sync.dma_start(out=out[:, cols], in_=mask[:, cols])
